import numpy as np
import ml_dtypes


def mxq(x, axis, fmt="e4m3"):
    dtype, down = {"e4m3": (ml_dtypes.float8_e4m3fn, 7), "e5m2": (ml_dtypes.float8_e5m2, 14)}[fmt]
    v = np.moveaxis(np.asarray(x, np.float32).astype(ml_dtypes.bfloat16).astype(np.float64), axis, -1)
    blocks = v.reshape(v.shape[:-1] + (-1, 32))
    amax = np.abs(blocks).max(-1, keepdims=True)
    byte = np.maximum(np.where(amax > 0, np.frexp(amax)[1] - 1 + 127, 0) - down, 1)
    scale = np.exp2(byte - 127.0)
    codes = (blocks / scale).astype(np.float32).astype(dtype).astype(np.float64)
    return np.moveaxis((codes * scale).reshape(v.shape), -1, axis)


WIDE = False


def mx_kscale(k):
    if not WIDE:
        return np.ones(k)
    levels = np.array([30, -30])
    if k % 512:
        return np.exp2(np.random.permutation(np.resize(levels, k // 32))).repeat(32)
    a = np.empty((k // 512, 16))
    for p in range(k // 512):
        a[p, :8] = np.random.permutation(np.resize(levels, 8))
        for g in range(8):
            far = levels[np.abs(levels - a[p, g]) >= 10]
            a[p, g + 8] = far[np.random.randint(len(far))]
    return np.exp2(a.ravel()).repeat(32)


def f64(x):
    return np.asarray(x).astype(np.float64)


def striped(idx):
    return np.tile(np.asarray(idx).reshape(-1, 16).T, (8, 1)).astype(np.uint16)


def unstriped(offs):
    return offs[:16].T.reshape(-1).astype(np.int64)


E2M1 = np.array([0.0, 0.5, 1.0, 1.5, 2.0, 3.0, 4.0, 6.0, -0.0, -0.5, -1.0, -1.5, -2.0, -3.0, -4.0, -6.0])


def pack_weight(w, fmt):
    k, n = w.shape
    w = f64(np.asarray(w, np.float32).astype(ml_dtypes.bfloat16)).reshape(k // 32, 32, n)
    amax = np.abs(w).max(1)
    if fmt in ("e4m3", "e5m2"):
        byte = np.frexp(amax)[1] - 1 + 127 - (7 if fmt == "e4m3" else 14)
    else:
        mant, ex = np.frexp(amax / 6.0)
        byte = np.where(mant > 0.5, ex, ex - 1) + 127
    byte = np.clip(np.where(amax > 0, byte, 1), 1, 254)
    scaled = (w * np.exp2(127.0 - byte)[:, None, :]).reshape(k, n).astype(np.float32)
    by_word = np.ascontiguousarray(scaled.reshape(k // 512, 128, 4, n).transpose(0, 1, 3, 2))
    if fmt in ("e4m3", "e5m2"):
        words = by_word.astype(ml_dtypes.float8_e4m3fn if fmt == "e4m3" else ml_dtypes.float8_e5m2).view(np.uint8)
    else:
        c = by_word.astype(ml_dtypes.float4_e2m1fn).view(np.uint8) & 0xF
        words = (c[..., 0::2] | (c[..., 1::2] << 4)).reshape(k // 512, 128, 2 * n)
    return np.ascontiguousarray(words), np.ascontiguousarray(byte.astype(np.uint8).reshape(k // 512, 16, n))


def unpack_weight(words, scales, fmt):
    g, _, n = scales.shape
    words = np.ascontiguousarray(words).reshape(g, 128, n, -1)
    if fmt in ("e4m3", "e5m2"):
        vals = words.view(ml_dtypes.float8_e4m3fn if fmt == "e4m3" else ml_dtypes.float8_e5m2).astype(np.float64)
    else:
        nib = np.empty((g, 128, n, 4), np.uint8)
        nib[..., 0::2] = words & 0xF
        nib[..., 1::2] = words >> 4
        vals = E2M1[nib]
    vals = vals * np.repeat(np.exp2(scales.astype(np.float64) - 127.0), 8, axis=1)[..., None]
    return vals.transpose(0, 1, 3, 2).reshape(g * 512, n)


K, F, T, Z, J, R, V, N, E = 512, 512, 1024, 1024, 256, 512, 1024, 256, 1024


def setup_inputs():
    n = np.random.standard_normal
    idx = np.random.permutation(T)[:J]
    idx2 = np.random.permutation(Z)[:J]
    idx3 = np.random.permutation(V)[:J]
    idx4 = np.random.permutation(T)[:J]
    idx5 = np.random.permutation(E)[:J]
    fk = mx_kscale(K)
    fr = mx_kscale(R)
    ff = mx_kscale(F)
    xtp = pack_weight(n((K, T)) / fk[:, None], "e5m2")
    wp = pack_weight(n((K, R)) * 1 / np.sqrt(K) * fk[:, None] * fr, "e2m1")
    xop = pack_weight(n((F, Z)) / ff[:, None], "e4m3")
    w0p = pack_weight(n((F, R)) * 1 / np.sqrt(F) * ff[:, None] * fr, "e2m1")
    wbp = pack_weight(n((R, N)) * 1 / np.sqrt(R) / fr[:, None], "e2m1")
    wsp = pack_weight(n((K, N)) * 1 / np.sqrt(K) * fk[:, None], "e2m1")
    return {
        "xt_words": xtp[0],
        "xt_scales": xtp[1],
        "w_words": wp[0],
        "w_scales": wp[1],
        "xo_words": xop[0],
        "xo_scales": xop[1],
        "w0_words": w0p[0],
        "w0_scales": w0p[1],
        "tb": (np.random.randint(-9, 10, (R, V)).astype(np.float64)).astype(np.float32),
        "st": (np.random.uniform(0.12, 0.3, (R, 1)) * fr[:, None]).astype(np.float32),
        "wb_words": wbp[0],
        "wb_scales": wbp[1],
        "ws_words": wsp[0],
        "ws_scales": wsp[1],
        "offs": striped(idx),
        "offs2": striped(idx2),
        "offs3": striped(idx3),
        "offs4": striped(idx4),
        "offs5": striped(idx5),
    }


def reference(xt_words, xt_scales, w_words, w_scales, xo_words, xo_scales, w0_words, w0_scales, tb, st, wb_words, wb_scales, ws_words, ws_scales, offs, offs2, offs3, offs4, offs5):
    idx = unstriped(offs)
    idx2 = unstriped(offs2)
    idx3 = unstriped(offs3)
    idx4 = unstriped(offs4)
    idx5 = unstriped(offs5)
    xtu = unpack_weight(xt_words, xt_scales, "e5m2")
    wu = unpack_weight(w_words, w_scales, "e2m1")
    xou = unpack_weight(xo_words, xo_scales, "e4m3")
    w0u = unpack_weight(w0_words, w0_scales, "e2m1")
    wbu = unpack_weight(wb_words, wb_scales, "e2m1")
    wsu = unpack_weight(ws_words, ws_scales, "e2m1")
    xtidxg = xtu[:, idx]
    xoidx2g = xou[:, idx2]
    a = wu.T @ xtidxg + w0u.T @ xoidx2g
    hid = np.maximum(a, f64(tb)[:, idx3] * f64(st))
    hidq = mxq(hid, 0, "e4m3")
    xtidx4g = xtu[:, idx4]
    p = wbu.T @ hidq + wsu.T @ xtidx4g
    y = np.zeros((N, E))
    y[:, idx5] = p
    return y

@@ -1,0 +1,220 @@
+from contextlib import ExitStack
+
+import concourse.mybir as mybir
+
+K, T, J, R, V, N, E = 512, 1024, 256, 512, 1024, 256, 1024
+FLOPS = 2 * K * R * J * 2 + 2 * R * N * J + 2 * K * N * J
+
+F32 = mybir.dt.float32
+BF16 = mybir.dt.bfloat16
+I32 = mybir.dt.int32
+U32 = mybir.dt.uint32
+U16 = mybir.dt.uint16
+U8 = mybir.dt.uint8
+E4M3 = mybir.dt.float8_e4m3fn_x4
+E5M2 = mybir.dt.float8_e5m2_x4
+E2M1 = mybir.dt.float4_e2m1fn_x4
+COPY = mybir.ActivationFunctionType.Copy
+MAX = mybir.AluOpType.max
+
+P = 128
+PACK = 4
+HALF = J // 2
+LIST_COLS = J // 16
+
+
+def load_scale_rows(queue, stage, first, scales):
+    rows = scales[0].rearrange("(h g r) c -> g r h c", h=2, g=2, r=4)
+    for g in range(2):
+        start = first + 32 * g
+        queue.dma_start(out=stage[start : start + 4].bitcast(I32), in_=rows[g].bitcast(I32))
+
+
+def tile_list_steptable_bank_further_scattered_kernel(
+    tc, xt_words, xt_scales, w_words, w_scales, xo_words, xo_scales, w0_words, w0_scales, tb, st,
+    wb_words, wb_scales, ws_words, ws_scales, offs, offs2, offs3, offs4, offs5, out,
+):
+    nc = tc.nc
+    with ExitStack() as ctx:
+        lists = ctx.enter_context(tc.tile_pool(name="lists", bufs=1))
+        keep = ctx.enter_context(tc.tile_pool(name="keep", bufs=1))
+        psum = ctx.enter_context(tc.psum_pool(name="psum", bufs=1))
+
+        def sb(name, shape, dtype):
+            return keep.tile(shape, dtype, name=name, align_bytes=64)
+
+        idx = lists.tile([P, LIST_COLS], U16, name="idx")
+        idx2 = lists.tile([P, LIST_COLS], U16, name="idx2")
+        idx3 = lists.tile([P, LIST_COLS], U16, name="idx3")
+        idx4 = lists.tile([P, LIST_COLS], U16, name="idx4")
+        idx5 = lists.tile([P, LIST_COLS], U16, name="idx5")
+
+        xt_w = sb("xt_w", [P, T], I32)
+        xo_w = sb("xo_w", [P, T], I32)
+        xt_stage = sb("xt_stage", [P, 2, T], U8)
+        xo_stage = sb("xo_stage", [P, 2, T], U8)
+        xt_s = sb("xt_s", [P, T], U8)
+        xo_s = sb("xo_s", [P, T], U8)
+        w_w = sb("w_w", [P, 2 * R], U8)
+        w0_w = sb("w0_w", [P, 2 * R], U8)
+        w_s = sb("w_s", [P, 2, R], U8)
+        w0_s = sb("w0_s", [P, 2, R], U8)
+        wb_w = sb("wb_w", [P, 2 * N], U8)
+        ws_w = sb("ws_w", [P, 2 * N], U8)
+        out_s = sb("out_s", [P, 2, 2 * N], U8)
+        steps = sb("steps", [P, PACK], F32)
+        table = [sb("table%d" % t, [P, V], F32) for t in range(PACK)]
+        pages = [sb("page%d" % n, [P, E], F32) for n in range(2)]
+
+        nc.vector.memset(xt_stage[64:128].bitcast(I32), 0)
+        nc.vector.memset(xo_stage[64:128].bitcast(I32), 0)
+        nc.vector.memset(w_s[:].bitcast(I32), 0)
+        nc.vector.memset(w0_s[:].bitcast(I32), 0)
+        nc.vector.memset(out_s[:].bitcast(I32), 0)
+        for n in range(2):
+            nc.vector.memset(pages[n][:], 0.0)
+
+        tb_rows = tb.rearrange("(p t) v -> t p v", t=PACK)
+        nc.sync.dma_start(idx[:], offs)
+        nc.sync.dma_start(out=xt_w[:], in_=xt_words[0].rearrange("p c r -> p (c r)").bitcast(I32))
+        load_scale_rows(nc.sync, xt_stage, 64, xt_scales)
+        nc.sync.dma_start(idx2[:], offs2)
+        load_scale_rows(nc.sync, xo_stage, 64, xo_scales)
+        nc.sync.dma_start(out=xo_w[:], in_=xo_words[0].rearrange("p c r -> p (c r)").bitcast(I32))
+        nc.sync.dma_start(out=w_w[:].bitcast(I32), in_=w_words[0].bitcast(I32))
+        load_scale_rows(nc.sync, w_s, 0, w_scales)
+        nc.sync.dma_start(out=w0_w[:].bitcast(I32), in_=w0_words[0].bitcast(I32))
+        load_scale_rows(nc.sync, w0_s, 0, w0_scales)
+        nc.sync.dma_start(out=table[0][:], in_=tb_rows[0])
+        nc.sync.dma_start(idx3[:], offs3)
+        nc.sync.dma_start(out=steps[:], in_=st.rearrange("(p t) o -> p (t o)", t=PACK))
+        nc.sync.dma_start(out=table[1][:], in_=tb_rows[1])
+        nc.sync.dma_start(idx4[:], offs4)
+        nc.sync.dma_start(out=table[2][:], in_=tb_rows[2])
+        load_scale_rows(nc.sync, out_s[:, :, 0:N], 0, wb_scales)
+        load_scale_rows(nc.sync, out_s[:, :, N : 2 * N], 0, ws_scales)
+        nc.sync.dma_start(out=table[3][:], in_=tb_rows[3])
+        nc.sync.dma_start(out=ws_w[:].bitcast(I32), in_=ws_words[0].bitcast(I32))
+        nc.sync.dma_start(out=wb_w[:].bitcast(I32), in_=wb_words[0].bitcast(I32))
+        nc.sync.dma_start(idx5[:], offs5)
+
+        def spread_token_scales(plane, stage):
+            for h in range(2):
+                nc.vector.tensor_copy(out=plane[64 * h : 64 * h + 64].bitcast(I32), in_=stage[64:128, h, :].bitcast(I32))
+
+        def spread_weight_scales(plane):
+            nc.vector.tensor_copy(out=plane[64:128, 0, :].bitcast(I32), in_=plane[0:64, 1, :].bitcast(I32))
+
+        def gather_words(name, words, offsets):
+            picked = sb(name, [P, J], U32)
+            nc.vector.tensor_copy(picked[:], words[:].bitcast(U32).indirect(offsets[:]))
+            return picked
+
+        def gather_scales(name, plane, offsets):
+            picked = sb(name, [P, J], U8)
+            nc.vector.tensor_copy(picked[:], plane[:].indirect(offsets[:]))
+            return picked
+
+        def deal_words(name, words):
+            dealt = sb(name, [P, 2 * R], U8)
+            nc.scalar.copy(
+                out=dealt[:].bitcast(U16).rearrange("p (t m) -> p t m", t=PACK),
+                in_=words[:].bitcast(U16).rearrange("p (m t) -> p t m", t=PACK),
+            )
+            return dealt
+
+        def deal_scales(name, plane):
+            dealt = sb(name, [P, R], U8)
+            nc.vector.tensor_copy(
+                out=dealt[:].rearrange("p (t m) -> p t m", t=PACK),
+                in_=plane[:, 0, :].rearrange("p (m t) -> p t m", t=PACK),
+            )
+            return dealt
+
+        xt1_w = gather_words("xt1_w", xt_w, idx)
+        spread_token_scales(xt_s, xt_stage)
+        spread_token_scales(xo_s, xo_stage)
+        xt1_s = gather_scales("xt1_s", xt_s, idx)
+        xo2_s = gather_scales("xo2_s", xo_s, idx2)
+        xo2_w = gather_words("xo2_w", xo_w, idx2)
+        spread_weight_scales(w_s)
+        w_dw = deal_words("w_dw", w_w)
+        w_ds = deal_scales("w_ds", w_s)
+        spread_weight_scales(w0_s)
+        w0_dw = deal_words("w0_dw", w0_w)
+        w0_ds = deal_scales("w0_ds", w0_s)
+
+        acc = [psum.tile([P, J], F32, name="acc%d" % t) for t in range(PACK)]
+        for dw, ds, xw, xs, fmt, first in ((w_dw, w_ds, xt1_w, xt1_s, E5M2, True), (w0_dw, w0_ds, xo2_w, xo2_s, E4M3, False)):
+            for t in range(PACK):
+                nc.tensor.matmul_mx(
+                    out=acc[t][:],
+                    lhsT=dw[:, 2 * P * t : 2 * P * (t + 1)].bitcast(E2M1),
+                    lhsT_scale=ds[:, P * t : P * (t + 1)],
+                    rhs=xw[:].bitcast(fmt),
+                    rhs_scale=xs[:],
+                    start=first,
+                    stop=not first,
+                )
+
+        xt4_w = gather_words("xt4_w", xt_w, idx4)
+        xt4_s = gather_scales("xt4_s", xt_s, idx4)
+
+        early = sb("early", [P, PACK - 1, J], BF16)
+        for t in range(PACK - 1):
+            level = sb("level%d" % t, [P, J], F32)
+            nc.scalar.activation(level[:], table[t][:].indirect(idx3[:]), COPY, scale=steps[:, t : t + 1])
+            nc.vector.tensor_tensor(early[:, t, :], acc[t][:], level[:], MAX)
+        spread_weight_scales(out_s)
+        hid = [sb("hid%d" % h, [P, HALF, PACK], BF16) for h in range(2)]
+        for h in range(2):
+            nc.vector.tensor_copy(
+                out=hid[h][:, :, 0 : PACK - 1],
+                in_=early[:, :, HALF * h : HALF * (h + 1)].rearrange("p t j -> p j t"),
+            )
+
+        sums = [[psum.tile([P, HALF], F32, name="sum%d%d" % (n, h)) for h in range(2)] for n in range(2)]
+        for h in range(2):
+            cols = slice(HALF * h, HALF * (h + 1))
+            for n in range(2):
+                nc.tensor.matmul_mx(
+                    out=sums[n][h][:],
+                    lhsT=ws_w[:, 2 * P * n : 2 * P * (n + 1)].bitcast(E2M1),
+                    lhsT_scale=out_s[:, 0, N + P * n : N + P * (n + 1)],
+                    rhs=xt4_w[:, cols].bitcast(E5M2),
+                    rhs_scale=xt4_s[:, cols],
+                    start=True,
+                    stop=False,
+                )
+
+        last = PACK - 1
+        for h in range(2):
+            level = sb("level%d%d" % (last, h), [P, HALF], F32)
+            nc.scalar.activation(
+                level[:], table[last][:].indirect(idx3[:, 8 * h : 8 * (h + 1)]), COPY, scale=steps[:, last : last + 1]
+            )
+            nc.vector.tensor_tensor(hid[h][:, :, last], acc[last][:, HALF * h : HALF * (h + 1)], level[:], MAX)
+        for h in range(2):
+            codes = sb("codes%d" % h, [P, HALF], U32)
+            plane = sb("plane%d" % h, [P, HALF], U8)
+            nc.vector.quantize_mx(out=codes[:].bitcast(E4M3), scales=plane[:], in_=hid[h][:].rearrange("p j t -> p (j t)"))
+            for n in range(2):
+                nc.tensor.matmul_mx(
+                    out=sums[n][h][:],
+                    lhsT=wb_w[:, 2 * P * n : 2 * P * (n + 1)].bitcast(E2M1),
+                    lhsT_scale=out_s[:, 0, P * n : P * (n + 1)],
+                    rhs=codes[:].bitcast(E4M3),
+                    rhs_scale=plane[:],
+                    start=False,
+                    stop=True,
+                )
+        for h in range(2):
+            places = idx5[:, 8 * h : 8 * (h + 1)]
+            low = sb("low%d" % h, [P, HALF], F32)
+            nc.scalar.copy(out=low[:], in_=sums[0][h][:])
+            nc.scalar.activation(pages[0][:].indirect(places), low[:], COPY)
+            high = sb("high%d" % h, [P, HALF], F32)
+            nc.vector.tensor_copy(out=high[:], in_=sums[1][h][:])
+            nc.vector.tensor_copy(pages[1][:].indirect(places), high[:])
+        nc.scalar.dma_start(out=out[0:P, :], in_=pages[0][:])
+        nc.sync.dma_start(out=out[P : 2 * P, :], in_=pages[1][:])

@@ -57,8 +57,7 @@ def tile_list_steptable_bank_further_scattered_kernel(
         xo_s = sb("xo_s", [P, T], U8)
         w_w = sb("w_w", [P, 2 * R], U8)
         w0_w = sb("w0_w", [P, 2 * R], U8)
-        w_s = sb("w_s", [P, 2, R], U8)
-        w0_s = sb("w0_s", [P, 2, R], U8)
+        in_s = sb("in_s", [P, 4, 2 * R], U8)
         wb_w = sb("wb_w", [P, 2 * N], U8)
         ws_w = sb("ws_w", [P, 2 * N], U8)
         out_s = sb("out_s", [P, 2, 2 * N], U8)
@@ -66,44 +65,40 @@ def tile_list_steptable_bank_further_scattered_kernel(
         table = [sb("table%d" % t, [P, V], F32) for t in range(PACK)]
         pages = [sb("page%d" % n, [P, E], F32) for n in range(2)]
 
-        nc.vector.memset(xt_stage[64:128].bitcast(I32), 0)
+        nc.vector.memset(xt_stage[0:64, 0, :].bitcast(I32), 0)
+        nc.gpsimd.memset(xt_stage[0:64, 1, :].bitcast(I32), 0)
+        nc.vector.memset(in_s[:, 0, :].bitcast(I32), 0)
         nc.vector.memset(xo_stage[64:128].bitcast(I32), 0)
-        nc.vector.memset(w_s[:].bitcast(I32), 0)
-        nc.vector.memset(w0_s[:].bitcast(I32), 0)
-        nc.vector.memset(out_s[:].bitcast(I32), 0)
-        for n in range(2):
-            nc.vector.memset(pages[n][:], 0.0)
+        nc.vector.memset(pages[0][:], 0.0)
+        nc.gpsimd.memset(out_s[:].bitcast(I32), 0)
+        nc.gpsimd.memset(pages[1][:], 0.0)
+
+        def load_scale_quarters(stage, scales):
+            nc.sync.dma_start(out=stage[0:4].bitcast(I32), in_=scales[0].rearrange("(q r) c -> r q c", r=4).bitcast(I32))
 
         tb_rows = tb.rearrange("(p t) v -> t p v", t=PACK)
         nc.sync.dma_start(idx[:], offs)
         nc.sync.dma_start(out=xt_w[:], in_=xt_words[0].rearrange("p c r -> p (c r)").bitcast(I32))
-        load_scale_rows(nc.sync, xt_stage, 64, xt_scales)
         nc.sync.dma_start(idx2[:], offs2)
-        load_scale_rows(nc.sync, xo_stage, 64, xo_scales)
-        nc.sync.dma_start(out=xo_w[:], in_=xo_words[0].rearrange("p c r -> p (c r)").bitcast(I32))
         nc.sync.dma_start(out=w_w[:].bitcast(I32), in_=w_words[0].bitcast(I32))
-        load_scale_rows(nc.sync, w_s, 0, w_scales)
-        nc.sync.dma_start(out=w0_w[:].bitcast(I32), in_=w0_words[0].bitcast(I32))
-        load_scale_rows(nc.sync, w0_s, 0, w0_scales)
+        load_scale_rows(nc.sync, xt_stage, 0, xt_scales)
+        load_scale_quarters(in_s[:, :, 0:R], w_scales)
+        load_scale_quarters(in_s[:, :, R : 2 * R], w0_scales)
+        nc.sync.dma_start(out=xo_w[:], in_=xo_words[0].rearrange("p c r -> p (c r)").bitcast(I32))
         nc.sync.dma_start(out=table[0][:], in_=tb_rows[0])
+        load_scale_rows(nc.sync, xo_stage, 64, xo_scales)
+        nc.sync.dma_start(out=w0_w[:].bitcast(I32), in_=w0_words[0].bitcast(I32))
         nc.sync.dma_start(idx3[:], offs3)
         nc.sync.dma_start(out=steps[:], in_=st.rearrange("(p t) o -> p (t o)", t=PACK))
         nc.sync.dma_start(out=table[1][:], in_=tb_rows[1])
-        nc.sync.dma_start(idx4[:], offs4)
         nc.sync.dma_start(out=table[2][:], in_=tb_rows[2])
-        load_scale_rows(nc.sync, out_s[:, :, 0:N], 0, wb_scales)
-        load_scale_rows(nc.sync, out_s[:, :, N : 2 * N], 0, ws_scales)
+        nc.sync.dma_start(idx4[:], offs4)
+        load_scale_rows(nc.sync, out_s[:, :, 0:N], 64, wb_scales)
+        load_scale_rows(nc.sync, out_s[:, :, N : 2 * N], 64, ws_scales)
         nc.sync.dma_start(out=table[3][:], in_=tb_rows[3])
         nc.sync.dma_start(out=ws_w[:].bitcast(I32), in_=ws_words[0].bitcast(I32))
         nc.sync.dma_start(out=wb_w[:].bitcast(I32), in_=wb_words[0].bitcast(I32))
         nc.sync.dma_start(idx5[:], offs5)
-
-        def spread_token_scales(plane, stage):
-            for h in range(2):
-                nc.vector.tensor_copy(out=plane[64 * h : 64 * h + 64].bitcast(I32), in_=stage[64:128, h, :].bitcast(I32))
-
-        def spread_weight_scales(plane):
-            nc.vector.tensor_copy(out=plane[64:128, 0, :].bitcast(I32), in_=plane[0:64, 1, :].bitcast(I32))
 
         def gather_words(name, words, offsets):
             picked = sb(name, [P, J], U32)
@@ -127,51 +122,59 @@ def tile_list_steptable_bank_further_scattered_kernel(
             dealt = sb(name, [P, R], U8)
             nc.vector.tensor_copy(
                 out=dealt[:].rearrange("p (t m) -> p t m", t=PACK),
-                in_=plane[:, 0, :].rearrange("p (m t) -> p t m", t=PACK),
+                in_=plane.rearrange("p (m t) -> p t m", t=PACK),
             )
             return dealt
 
         xt1_w = gather_words("xt1_w", xt_w, idx)
-        spread_token_scales(xt_s, xt_stage)
-        spread_token_scales(xo_s, xo_stage)
+        for h in range(2):
+            nc.vector.tensor_copy(out=xt_s[64 * h : 64 * h + 64].bitcast(I32), in_=xt_stage[0:64, h, :].bitcast(I32))
+        for q in range(1, 4):
+            nc.vector.tensor_copy(out=in_s[32 * q : 32 * q + 4, 0, :].bitcast(I32), in_=in_s[0:4, q, :].bitcast(I32))
         xt1_s = gather_scales("xt1_s", xt_s, idx)
-        xo2_s = gather_scales("xo2_s", xo_s, idx2)
-        xo2_w = gather_words("xo2_w", xo_w, idx2)
-        spread_weight_scales(w_s)
         w_dw = deal_words("w_dw", w_w)
-        w_ds = deal_scales("w_ds", w_s)
-        spread_weight_scales(w0_s)
         w0_dw = deal_words("w0_dw", w0_w)
-        w0_ds = deal_scales("w0_ds", w0_s)
+        w_ds = deal_scales("w_ds", in_s[:, 0, 0:R])
+        w0_ds = deal_scales("w0_ds", in_s[:, 0, R : 2 * R])
+        for h in range(2):
+            nc.vector.tensor_copy(out=xo_s[64 * h : 64 * h + 64].bitcast(I32), in_=xo_stage[64:128, h, :].bitcast(I32))
+        xo2_w = gather_words("xo2_w", xo_w, idx2)
+        xo2_s = gather_scales("xo2_s", xo_s, idx2)
 
-        acc = [psum.tile([P, J], F32, name="acc%d" % t) for t in range(PACK)]
+        acc = [psum.tile([P, 2, J], F32, name="acc%d" % u) for u in range(2)]
         for dw, ds, xw, xs, fmt, first in ((w_dw, w_ds, xt1_w, xt1_s, E5M2, True), (w0_dw, w0_ds, xo2_w, xo2_s, E4M3, False)):
             for t in range(PACK):
                 nc.tensor.matmul_mx(
-                    out=acc[t][:],
+                    out=acc[t // 2][:, t % 2, :],
                     lhsT=dw[:, 2 * P * t : 2 * P * (t + 1)].bitcast(E2M1),
                     lhsT_scale=ds[:, P * t : P * (t + 1)],
                     rhs=xw[:].bitcast(fmt),
                     rhs_scale=xs[:],
-                    start=first,
-                    stop=not first,
+                    start=first and t % 2 == 0,
+                    stop=not first and t % 2 == 1,
                 )
-
         xt4_w = gather_words("xt4_w", xt_w, idx4)
         xt4_s = gather_scales("xt4_s", xt_s, idx4)
+        nc.vector.tensor_copy(out=out_s[0:64, 1, :].bitcast(I32), in_=out_s[64:128, 0, :].bitcast(I32))
 
-        early = sb("early", [P, PACK - 1, J], BF16)
-        for t in range(PACK - 1):
-            level = sb("level%d" % t, [P, J], F32)
-            nc.scalar.activation(level[:], table[t][:].indirect(idx3[:]), COPY, scale=steps[:, t : t + 1])
-            nc.vector.tensor_tensor(early[:, t, :], acc[t][:], level[:], MAX)
-        spread_weight_scales(out_s)
         hid = [sb("hid%d" % h, [P, HALF, PACK], BF16) for h in range(2)]
+        low_levels = sb("low_levels", [P, 2, J], F32)
+        for t in range(2):
+            nc.scalar.activation(low_levels[:, t, :], table[t][:].indirect(idx3[:]), COPY, scale=steps[:, t : t + 1])
         for h in range(2):
-            nc.vector.tensor_copy(
-                out=hid[h][:, :, 0 : PACK - 1],
-                in_=early[:, :, HALF * h : HALF * (h + 1)].rearrange("p t j -> p j t"),
+            cols = slice(HALF * h, HALF * (h + 1))
+            nc.vector.tensor_tensor(
+                hid[h][:, :, 0:2],
+                acc[0][:, :, cols].rearrange("p t j -> p j t"),
+                low_levels[:, :, cols].rearrange("p t j -> p j t"),
+                MAX,
             )
+        high_levels = [sb("high_levels%d" % h, [P, 2, HALF], F32) for h in range(2)]
+        for t in range(2, PACK):
+            for h in range(2):
+                nc.scalar.activation(
+                    high_levels[h][:, t - 2, :], table[t][:].indirect(idx3[:, 8 * h : 8 * (h + 1)]), COPY, scale=steps[:, t : t + 1]
+                )
 
         sums = [[psum.tile([P, HALF], F32, name="sum%d%d" % (n, h)) for h in range(2)] for n in range(2)]
         for h in range(2):
@@ -180,20 +183,20 @@ def tile_list_steptable_bank_further_scattered_kernel(
                 nc.tensor.matmul_mx(
                     out=sums[n][h][:],
                     lhsT=ws_w[:, 2 * P * n : 2 * P * (n + 1)].bitcast(E2M1),
-                    lhsT_scale=out_s[:, 0, N + P * n : N + P * (n + 1)],
+                    lhsT_scale=out_s[:, 1, N + P * n : N + P * (n + 1)],
                     rhs=xt4_w[:, cols].bitcast(E5M2),
                     rhs_scale=xt4_s[:, cols],
                     start=True,
                     stop=False,
                 )
 
-        last = PACK - 1
         for h in range(2):
-            level = sb("level%d%d" % (last, h), [P, HALF], F32)
-            nc.scalar.activation(
-                level[:], table[last][:].indirect(idx3[:, 8 * h : 8 * (h + 1)]), COPY, scale=steps[:, last : last + 1]
+            nc.vector.tensor_tensor(
+                hid[h][:, :, 2:PACK],
+                acc[1][:, :, HALF * h : HALF * (h + 1)].rearrange("p t j -> p j t"),
+                high_levels[h][:].rearrange("p t j -> p j t"),
+                MAX,
             )
-            nc.vector.tensor_tensor(hid[h][:, :, last], acc[last][:, HALF * h : HALF * (h + 1)], level[:], MAX)
         for h in range(2):
             codes = sb("codes%d" % h, [P, HALF], U32)
             plane = sb("plane%d" % h, [P, HALF], U8)
@@ -202,7 +205,7 @@ def tile_list_steptable_bank_further_scattered_kernel(
                 nc.tensor.matmul_mx(
                     out=sums[n][h][:],
                     lhsT=wb_w[:, 2 * P * n : 2 * P * (n + 1)].bitcast(E2M1),
-                    lhsT_scale=out_s[:, 0, P * n : P * (n + 1)],
+                    lhsT_scale=out_s[:, 1, P * n : P * (n + 1)],
                     rhs=codes[:].bitcast(E4M3),
                     rhs_scale=plane[:],
                     start=False,

@@ -30,6 +30,12 @@ def load_scale_rows(queue, stage, first, scales):
         queue.dma_start(out=stage[start : start + 4].bitcast(I32), in_=rows[g].bitcast(I32))
 
 
+def load_scale_plane(queue, plane, scales):
+    rows = scales[0].rearrange("(q r) c -> r q c", r=4)
+    for r in range(4):
+        queue.dma_start(out=plane[r:P:32, :].bitcast(I32), in_=rows[r].bitcast(I32))
+
+
 def tile_list_steptable_bank_further_scattered_kernel(
     tc, xt_words, xt_scales, w_words, w_scales, xo_words, xo_scales, w0_words, w0_scales, tb, st,
     wb_words, wb_scales, ws_words, ws_scales, offs, offs2, offs3, offs4, offs5, out,
@@ -60,7 +66,7 @@ def tile_list_steptable_bank_further_scattered_kernel(
         in_s = sb("in_s", [P, 4, 2 * R], U8)
         wb_w = sb("wb_w", [P, 2 * N], U8)
         ws_w = sb("ws_w", [P, 2 * N], U8)
-        out_s = sb("out_s", [P, 2, 2 * N], U8)
+        out_s = sb("out_s", [P, 2 * N], U8)
         steps = sb("steps", [P, PACK], F32)
         table = [sb("table%d" % t, [P, V], F32) for t in range(PACK)]
         pages = [sb("page%d" % n, [P, E], F32) for n in range(2)]
@@ -88,16 +94,16 @@ def tile_list_steptable_bank_further_scattered_kernel(
         nc.sync.dma_start(out=table[0][:], in_=tb_rows[0])
         load_scale_rows(nc.sync, xo_stage, 64, xo_scales)
         nc.sync.dma_start(out=w0_w[:].bitcast(I32), in_=w0_words[0].bitcast(I32))
+        nc.sync.dma_start(idx4[:], offs4)
         nc.sync.dma_start(idx3[:], offs3)
         nc.sync.dma_start(out=steps[:], in_=st.rearrange("(p t) o -> p (t o)", t=PACK))
         nc.sync.dma_start(out=table[1][:], in_=tb_rows[1])
         nc.sync.dma_start(out=table[2][:], in_=tb_rows[2])
-        nc.sync.dma_start(idx4[:], offs4)
-        load_scale_rows(nc.sync, out_s[:, :, 0:N], 64, wb_scales)
-        load_scale_rows(nc.sync, out_s[:, :, N : 2 * N], 64, ws_scales)
+        load_scale_plane(nc.sync, out_s[:, N : 2 * N], ws_scales)
         nc.sync.dma_start(out=table[3][:], in_=tb_rows[3])
         nc.sync.dma_start(out=ws_w[:].bitcast(I32), in_=ws_words[0].bitcast(I32))
         nc.sync.dma_start(out=wb_w[:].bitcast(I32), in_=wb_words[0].bitcast(I32))
+        load_scale_plane(nc.sync, out_s[:, 0:N], wb_scales)
         nc.sync.dma_start(idx5[:], offs5)
 
         def gather_words(name, words, offsets):
@@ -155,7 +161,6 @@ def tile_list_steptable_bank_further_scattered_kernel(
                 )
         xt4_w = gather_words("xt4_w", xt_w, idx4)
         xt4_s = gather_scales("xt4_s", xt_s, idx4)
-        nc.vector.tensor_copy(out=out_s[0:64, 1, :].bitcast(I32), in_=out_s[64:128, 0, :].bitcast(I32))
 
         hid = [sb("hid%d" % h, [P, HALF, PACK], BF16) for h in range(2)]
         low_levels = sb("low_levels", [P, 2, J], F32)
@@ -176,19 +181,19 @@ def tile_list_steptable_bank_further_scattered_kernel(
                     high_levels[h][:, t - 2, :], table[t][:].indirect(idx3[:, 8 * h : 8 * (h + 1)]), COPY, scale=steps[:, t : t + 1]
                 )
 
-        sums = [[psum.tile([P, HALF], F32, name="sum%d%d" % (n, h)) for h in range(2)] for n in range(2)]
-        for h in range(2):
-            cols = slice(HALF * h, HALF * (h + 1))
-            for n in range(2):
-                nc.tensor.matmul_mx(
-                    out=sums[n][h][:],
-                    lhsT=ws_w[:, 2 * P * n : 2 * P * (n + 1)].bitcast(E2M1),
-                    lhsT_scale=out_s[:, 1, N + P * n : N + P * (n + 1)],
-                    rhs=xt4_w[:, cols].bitcast(E5M2),
-                    rhs_scale=xt4_s[:, cols],
-                    start=True,
-                    stop=False,
-                )
+        low_sums = [psum.tile([P, HALF], F32, name="low_sum%d" % h) for h in range(2)]
+        high_sum = psum.tile([P, J], F32, name="high_sum")
+        pieces = [(low_sums[0], 0, slice(0, HALF)), (low_sums[1], 0, slice(HALF, J)), (high_sum, 1, slice(0, J))]
+        for total, n, cols in pieces:
+            nc.tensor.matmul_mx(
+                out=total[:],
+                lhsT=ws_w[:, 2 * P * n : 2 * P * (n + 1)].bitcast(E2M1),
+                lhsT_scale=out_s[:, N + P * n : N + P * (n + 1)],
+                rhs=xt4_w[:, cols].bitcast(E5M2),
+                rhs_scale=xt4_s[:, cols],
+                start=True,
+                stop=False,
+            )
 
         for h in range(2):
             nc.vector.tensor_tensor(
@@ -197,27 +202,28 @@ def tile_list_steptable_bank_further_scattered_kernel(
                 high_levels[h][:].rearrange("p t j -> p j t"),
                 MAX,
             )
+        codes = sb("codes", [P, J], U32)
+        plane = sb("plane", [P, J], U8)
         for h in range(2):
-            codes = sb("codes%d" % h, [P, HALF], U32)
-            plane = sb("plane%d" % h, [P, HALF], U8)
-            nc.vector.quantize_mx(out=codes[:].bitcast(E4M3), scales=plane[:], in_=hid[h][:].rearrange("p j t -> p (j t)"))
-            for n in range(2):
-                nc.tensor.matmul_mx(
-                    out=sums[n][h][:],
-                    lhsT=wb_w[:, 2 * P * n : 2 * P * (n + 1)].bitcast(E2M1),
-                    lhsT_scale=out_s[:, 1, P * n : P * (n + 1)],
-                    rhs=codes[:].bitcast(E4M3),
-                    rhs_scale=plane[:],
-                    start=False,
-                    stop=True,
-                )
+            cols = slice(HALF * h, HALF * (h + 1))
+            nc.vector.quantize_mx(out=codes[:, cols].bitcast(E4M3), scales=plane[:, cols], in_=hid[h][:].rearrange("p j t -> p (j t)"))
+        for total, n, cols in pieces:
+            nc.tensor.matmul_mx(
+                out=total[:],
+                lhsT=wb_w[:, 2 * P * n : 2 * P * (n + 1)].bitcast(E2M1),
+                lhsT_scale=out_s[:, P * n : P * (n + 1)],
+                rhs=codes[:, cols].bitcast(E4M3),
+                rhs_scale=plane[:, cols],
+                start=False,
+                stop=True,
+            )
+        low = [sb("low%d" % h, [P, HALF], F32) for h in range(2)]
+        high = sb("high", [P, J], F32)
+        nc.scalar.copy(out=low[0][:], in_=low_sums[0][:])
+        nc.vector.tensor_copy(out=low[1][:], in_=low_sums[1][:])
+        nc.vector.tensor_copy(out=high[:], in_=high_sum[:])
         for h in range(2):
-            places = idx5[:, 8 * h : 8 * (h + 1)]
-            low = sb("low%d" % h, [P, HALF], F32)
-            nc.scalar.copy(out=low[:], in_=sums[0][h][:])
-            nc.scalar.activation(pages[0][:].indirect(places), low[:], COPY)
-            high = sb("high%d" % h, [P, HALF], F32)
-            nc.vector.tensor_copy(out=high[:], in_=sums[1][h][:])
-            nc.vector.tensor_copy(pages[1][:].indirect(places), high[:])
+            nc.scalar.activation(pages[0][:].indirect(idx5[:, 8 * h : 8 * (h + 1)]), low[h][:], COPY)
+        nc.vector.tensor_copy(pages[1][:].indirect(idx5[:]), high[:])
         nc.scalar.dma_start(out=out[0:P, :], in_=pages[0][:])
         nc.sync.dma_start(out=out[P : 2 * P, :], in_=pages[1][:])

from contextlib import ExitStack

import concourse.mybir as mybir

K, T, J, R, V, N, E = 512, 1024, 256, 512, 1024, 256, 1024
FLOPS = 2 * K * R * J * 2 + 2 * R * N * J + 2 * K * N * J

F32 = mybir.dt.float32
BF16 = mybir.dt.bfloat16
I32 = mybir.dt.int32
U32 = mybir.dt.uint32
U16 = mybir.dt.uint16
U8 = mybir.dt.uint8
E4M3 = mybir.dt.float8_e4m3fn_x4
E5M2 = mybir.dt.float8_e5m2_x4
E2M1 = mybir.dt.float4_e2m1fn_x4
COPY = mybir.ActivationFunctionType.Copy
MAX = mybir.AluOpType.max

P = 128
PACK = 4
HALF = J // 2
LIST_COLS = J // 16


def load_scale_rows(queue, stage, first, scales):
    rows = scales[0].rearrange("(h g r) c -> g r h c", h=2, g=2, r=4)
    for g in range(2):
        start = first + 32 * g
        queue.dma_start(out=stage[start : start + 4].bitcast(I32), in_=rows[g].bitcast(I32))


def load_scale_plane(queue, plane, scales):
    rows = scales[0].rearrange("(q r) c -> r q c", r=4)
    for r in range(4):
        queue.dma_start(out=plane[r:P:32, :].bitcast(I32), in_=rows[r].bitcast(I32))


def tile_list_steptable_bank_further_scattered_kernel(
    tc, xt_words, xt_scales, w_words, w_scales, xo_words, xo_scales, w0_words, w0_scales, tb, st,
    wb_words, wb_scales, ws_words, ws_scales, offs, offs2, offs3, offs4, offs5, out,
):
    nc = tc.nc
    with ExitStack() as ctx:
        lists = ctx.enter_context(tc.tile_pool(name="lists", bufs=1))
        keep = ctx.enter_context(tc.tile_pool(name="keep", bufs=1))
        psum = ctx.enter_context(tc.psum_pool(name="psum", bufs=1))

        def sb(name, shape, dtype):
            return keep.tile(shape, dtype, name=name, align_bytes=64)

        idx = lists.tile([P, LIST_COLS], U16, name="idx")
        idx2 = lists.tile([P, LIST_COLS], U16, name="idx2")
        idx3 = lists.tile([P, LIST_COLS], U16, name="idx3")
        idx4 = lists.tile([P, LIST_COLS], U16, name="idx4")
        idx5 = lists.tile([P, LIST_COLS], U16, name="idx5")

        xt_w = sb("xt_w", [P, T], I32)
        xo_w = sb("xo_w", [P, T], I32)
        xt_stage = sb("xt_stage", [P, 2, T], U8)
        xo_stage = sb("xo_stage", [P, 2, T], U8)
        xt_s = sb("xt_s", [P, T], U8)
        xo_s = sb("xo_s", [P, T], U8)
        w_w = sb("w_w", [P, 2 * R], U8)
        w0_w = sb("w0_w", [P, 2 * R], U8)
        in_s = sb("in_s", [P, 4, 2 * R], U8)
        wb_w = sb("wb_w", [P, 2 * N], U8)
        ws_w = sb("ws_w", [P, 2 * N], U8)
        out_s = sb("out_s", [P, 2 * N], U8)
        steps = sb("steps", [P, PACK], F32)
        table = [sb("table%d" % t, [P, V], F32) for t in range(PACK)]
        pages = [sb("page%d" % n, [P, E], F32) for n in range(2)]

        nc.vector.memset(xt_stage[0:64, 0, :].bitcast(I32), 0)
        nc.gpsimd.memset(xt_stage[0:64, 1, :].bitcast(I32), 0)
        nc.vector.memset(in_s[:, 0, :].bitcast(I32), 0)
        nc.vector.memset(xo_stage[64:128].bitcast(I32), 0)
        nc.vector.memset(pages[0][:], 0.0)
        nc.gpsimd.memset(out_s[:].bitcast(I32), 0)
        nc.gpsimd.memset(pages[1][:], 0.0)

        def load_scale_quarters(stage, scales):
            nc.sync.dma_start(out=stage[0:4].bitcast(I32), in_=scales[0].rearrange("(q r) c -> r q c", r=4).bitcast(I32))

        tb_rows = tb.rearrange("(p t) v -> t p v", t=PACK)
        nc.sync.dma_start(idx[:], offs)
        nc.sync.dma_start(out=xt_w[:], in_=xt_words[0].rearrange("p c r -> p (c r)").bitcast(I32))
        nc.sync.dma_start(idx2[:], offs2)
        nc.sync.dma_start(out=w_w[:].bitcast(I32), in_=w_words[0].bitcast(I32))
        load_scale_rows(nc.sync, xt_stage, 0, xt_scales)
        load_scale_quarters(in_s[:, :, 0:R], w_scales)
        load_scale_quarters(in_s[:, :, R : 2 * R], w0_scales)
        nc.sync.dma_start(out=xo_w[:], in_=xo_words[0].rearrange("p c r -> p (c r)").bitcast(I32))
        nc.sync.dma_start(out=table[0][:], in_=tb_rows[0])
        load_scale_rows(nc.sync, xo_stage, 64, xo_scales)
        nc.sync.dma_start(out=w0_w[:].bitcast(I32), in_=w0_words[0].bitcast(I32))
        nc.sync.dma_start(idx4[:], offs4)
        nc.sync.dma_start(idx3[:], offs3)
        nc.sync.dma_start(out=steps[:], in_=st.rearrange("(p t) o -> p (t o)", t=PACK))
        nc.sync.dma_start(out=table[1][:], in_=tb_rows[1])
        nc.sync.dma_start(out=table[2][:], in_=tb_rows[2])
        load_scale_plane(nc.sync, out_s[:, N : 2 * N], ws_scales)
        nc.sync.dma_start(out=table[3][:], in_=tb_rows[3])
        nc.sync.dma_start(out=ws_w[:].bitcast(I32), in_=ws_words[0].bitcast(I32))
        nc.sync.dma_start(out=wb_w[:].bitcast(I32), in_=wb_words[0].bitcast(I32))
        load_scale_plane(nc.sync, out_s[:, 0:N], wb_scales)
        nc.sync.dma_start(idx5[:], offs5)

        def gather_words(name, words, offsets):
            picked = sb(name, [P, J], U32)
            nc.vector.tensor_copy(picked[:], words[:].bitcast(U32).indirect(offsets[:]))
            return picked

        def gather_scales(name, plane, offsets):
            picked = sb(name, [P, J], U8)
            nc.vector.tensor_copy(picked[:], plane[:].indirect(offsets[:]))
            return picked

        def deal_words(name, words):
            dealt = sb(name, [P, 2 * R], U8)
            nc.scalar.copy(
                out=dealt[:].bitcast(U16).rearrange("p (t m) -> p t m", t=PACK),
                in_=words[:].bitcast(U16).rearrange("p (m t) -> p t m", t=PACK),
            )
            return dealt

        def deal_scales(name, plane):
            dealt = sb(name, [P, R], U8)
            nc.vector.tensor_copy(
                out=dealt[:].rearrange("p (t m) -> p t m", t=PACK),
                in_=plane.rearrange("p (m t) -> p t m", t=PACK),
            )
            return dealt

        xt1_w = gather_words("xt1_w", xt_w, idx)
        for h in range(2):
            nc.vector.tensor_copy(out=xt_s[64 * h : 64 * h + 64].bitcast(I32), in_=xt_stage[0:64, h, :].bitcast(I32))
        for q in range(1, 4):
            nc.vector.tensor_copy(out=in_s[32 * q : 32 * q + 4, 0, :].bitcast(I32), in_=in_s[0:4, q, :].bitcast(I32))
        xt1_s = gather_scales("xt1_s", xt_s, idx)
        w_dw = deal_words("w_dw", w_w)
        w0_dw = deal_words("w0_dw", w0_w)
        w_ds = deal_scales("w_ds", in_s[:, 0, 0:R])
        w0_ds = deal_scales("w0_ds", in_s[:, 0, R : 2 * R])
        for h in range(2):
            nc.vector.tensor_copy(out=xo_s[64 * h : 64 * h + 64].bitcast(I32), in_=xo_stage[64:128, h, :].bitcast(I32))
        xo2_w = gather_words("xo2_w", xo_w, idx2)
        xo2_s = gather_scales("xo2_s", xo_s, idx2)

        acc = [psum.tile([P, 2, J], F32, name="acc%d" % u) for u in range(2)]
        for dw, ds, xw, xs, fmt, first in ((w_dw, w_ds, xt1_w, xt1_s, E5M2, True), (w0_dw, w0_ds, xo2_w, xo2_s, E4M3, False)):
            for t in range(PACK):
                nc.tensor.matmul_mx(
                    out=acc[t // 2][:, t % 2, :],
                    lhsT=dw[:, 2 * P * t : 2 * P * (t + 1)].bitcast(E2M1),
                    lhsT_scale=ds[:, P * t : P * (t + 1)],
                    rhs=xw[:].bitcast(fmt),
                    rhs_scale=xs[:],
                    start=first and t % 2 == 0,
                    stop=not first and t % 2 == 1,
                )
        xt4_w = gather_words("xt4_w", xt_w, idx4)
        xt4_s = gather_scales("xt4_s", xt_s, idx4)

        hid = [sb("hid%d" % h, [P, HALF, PACK], BF16) for h in range(2)]
        low_levels = sb("low_levels", [P, 2, J], F32)
        for t in range(2):
            nc.scalar.activation(low_levels[:, t, :], table[t][:].indirect(idx3[:]), COPY, scale=steps[:, t : t + 1])
        for h in range(2):
            cols = slice(HALF * h, HALF * (h + 1))
            nc.vector.tensor_tensor(
                hid[h][:, :, 0:2],
                acc[0][:, :, cols].rearrange("p t j -> p j t"),
                low_levels[:, :, cols].rearrange("p t j -> p j t"),
                MAX,
            )
        high_levels = [sb("high_levels%d" % h, [P, 2, HALF], F32) for h in range(2)]
        for t in range(2, PACK):
            for h in range(2):
                nc.scalar.activation(
                    high_levels[h][:, t - 2, :], table[t][:].indirect(idx3[:, 8 * h : 8 * (h + 1)]), COPY, scale=steps[:, t : t + 1]
                )

        low_sums = [psum.tile([P, HALF], F32, name="low_sum%d" % h) for h in range(2)]
        high_sum = psum.tile([P, J], F32, name="high_sum")
        pieces = [(low_sums[0], 0, slice(0, HALF)), (low_sums[1], 0, slice(HALF, J)), (high_sum, 1, slice(0, J))]
        for total, n, cols in pieces:
            nc.tensor.matmul_mx(
                out=total[:],
                lhsT=ws_w[:, 2 * P * n : 2 * P * (n + 1)].bitcast(E2M1),
                lhsT_scale=out_s[:, N + P * n : N + P * (n + 1)],
                rhs=xt4_w[:, cols].bitcast(E5M2),
                rhs_scale=xt4_s[:, cols],
                start=True,
                stop=False,
            )

        for h in range(2):
            nc.vector.tensor_tensor(
                hid[h][:, :, 2:PACK],
                acc[1][:, :, HALF * h : HALF * (h + 1)].rearrange("p t j -> p j t"),
                high_levels[h][:].rearrange("p t j -> p j t"),
                MAX,
            )
        codes = sb("codes", [P, J], U32)
        plane = sb("plane", [P, J], U8)
        for h in range(2):
            cols = slice(HALF * h, HALF * (h + 1))
            nc.vector.quantize_mx(out=codes[:, cols].bitcast(E4M3), scales=plane[:, cols], in_=hid[h][:].rearrange("p j t -> p (j t)"))
        for total, n, cols in pieces:
            nc.tensor.matmul_mx(
                out=total[:],
                lhsT=wb_w[:, 2 * P * n : 2 * P * (n + 1)].bitcast(E2M1),
                lhsT_scale=out_s[:, P * n : P * (n + 1)],
                rhs=codes[:, cols].bitcast(E4M3),
                rhs_scale=plane[:, cols],
                start=False,
                stop=True,
            )
        low = [sb("low%d" % h, [P, HALF], F32) for h in range(2)]
        high = sb("high", [P, J], F32)
        nc.scalar.copy(out=low[0][:], in_=low_sums[0][:])
        nc.vector.tensor_copy(out=low[1][:], in_=low_sums[1][:])
        nc.vector.tensor_copy(out=high[:], in_=high_sum[:])
        for h in range(2):
            nc.scalar.activation(pages[0][:].indirect(idx5[:, 8 * h : 8 * (h + 1)]), low[h][:], COPY)
        nc.vector.tensor_copy(pages[1][:].indirect(idx5[:]), high[:])
        nc.scalar.dma_start(out=out[0:P, :], in_=pages[0][:])
        nc.sync.dma_start(out=out[P : 2 * P, :], in_=pages[1][:])
